import numpy as np
import ml_dtypes


def mxq(x, axis, fmt="e4m3"):
    dtype, down = {"e4m3": (ml_dtypes.float8_e4m3fn, 7), "e5m2": (ml_dtypes.float8_e5m2, 14)}[fmt]
    v = np.moveaxis(np.asarray(x, np.float32).astype(ml_dtypes.bfloat16).astype(np.float64), axis, -1)
    blocks = v.reshape(v.shape[:-1] + (-1, 32))
    amax = np.abs(blocks).max(-1, keepdims=True)
    byte = np.maximum(np.where(amax > 0, np.frexp(amax)[1] - 1 + 127, 0) - down, 1)
    scale = np.exp2(byte - 127.0)
    codes = (blocks / scale).astype(np.float32).astype(dtype).astype(np.float64)
    return np.moveaxis((codes * scale).reshape(v.shape), -1, axis)


WIDE = False


def mx_kscale(k):
    if not WIDE:
        return np.ones(k)
    levels = np.array([10, -10, 5, -5, 0])
    if k % 512:
        return np.exp2(np.random.permutation(np.resize(levels, k // 32))).repeat(32)
    a = np.empty((k // 512, 16))
    for p in range(k // 512):
        a[p, :8] = np.random.permutation(np.resize(levels, 8))
        for g in range(8):
            far = levels[np.abs(levels - a[p, g]) >= 10]
            a[p, g + 8] = far[np.random.randint(len(far))]
    return np.exp2(a.ravel()).repeat(32)


def f64(x):
    return np.asarray(x).astype(np.float64)


def striped(idx):
    return np.tile(idx.reshape(-1, 16).T, (8, 1)).astype(np.uint16)


def unstriped(offs):
    return offs[:16].T.reshape(-1).astype(np.int64)


E2M1 = np.array([0.0, 0.5, 1.0, 1.5, 2.0, 3.0, 4.0, 6.0, -0.0, -0.5, -1.0, -1.5, -2.0, -3.0, -4.0, -6.0])


def pack_weight(w, fmt):
    k, n = w.shape
    w = f64(np.asarray(w, np.float32).astype(ml_dtypes.bfloat16)).reshape(k // 32, 32, n)
    amax = np.abs(w).max(1)
    if fmt == "e4m3":
        byte = np.frexp(amax)[1] - 1 + 127 - 7
    else:
        mant, ex = np.frexp(amax / 6.0)
        byte = np.where(mant > 0.5, ex, ex - 1) + 127
    byte = np.clip(np.where(amax > 0, byte, 1), 1, 254)
    scaled = (w * np.exp2(127.0 - byte)[:, None, :]).reshape(k, n).astype(np.float32)
    by_word = np.ascontiguousarray(scaled.reshape(k // 512, 128, 4, n).transpose(0, 1, 3, 2))
    if fmt == "e4m3":
        words = by_word.astype(ml_dtypes.float8_e4m3fn).view(np.uint8)
    else:
        c = by_word.astype(ml_dtypes.float4_e2m1fn).view(np.uint8) & 0xF
        words = (c[..., 0::2] | (c[..., 1::2] << 4)).reshape(k // 512, 128, 2 * n)
    return np.ascontiguousarray(words), np.ascontiguousarray(byte.astype(np.uint8).reshape(k // 512, 16, n))


def unpack_weight(words, scales, fmt):
    g, _, n = scales.shape
    words = np.ascontiguousarray(words).reshape(g, 128, n, -1)
    if fmt == "e4m3":
        vals = words.view(ml_dtypes.float8_e4m3fn).astype(np.float64)
    else:
        nib = np.empty((g, 128, n, 4), np.uint8)
        nib[..., 0::2] = words & 0xF
        nib[..., 1::2] = words >> 4
        vals = E2M1[nib]
    vals = vals * np.repeat(np.exp2(scales.astype(np.float64) - 127.0), 8, axis=1)[..., None]
    return vals.transpose(0, 1, 3, 2).reshape(g * 512, n)


def gelu(v):
    return 0.5 * v * (1.0 + np.tanh(np.sqrt(2.0 / np.pi) * (v + 0.044715 * v**3)))


def twice(P):
    return np.random.permutation(np.repeat(np.arange(P), 2))


K, T, S, P, H = 1024, 2048, 1024, 512, 1024

def setup_inputs():
    n = np.random.standard_normal
    s = mx_kscale(K)[:, None]
    u = mx_kscale(H)[:, None]
    d = {}
    d["tab_words"], d["tab_scales"] = pack_weight(n((K, T)) * s, "e4m3")
    d["offs"] = striped(np.random.permutation(T)[:S])
    d["pos1"] = striped(np.random.permutation(S)[:P])
    d["pos2"] = striped(np.random.permutation(S)[:P])
    d["pos3"] = striped(twice(P))
    d["w1"] = (n((K, H)) / K**0.5 / s * u.T).astype(np.float32)
    d["base"] = (0.8 * n((H, S)) * u).astype(np.float32)
    d["w2_words"], d["w2_scales"] = pack_weight(n((H, H)) / H**0.5 / u, "e2m1")
    d["gain"] = (np.exp(0.3 * n(H)) * u[:, 0]).astype(np.float32)
    d["w3"] = (2.0 * n((H, H)) / H**0.5 / u).astype(np.float32)
    d["hs"] = (1.3 * np.exp(0.3 * n(H)) / u[:, 0]).astype(np.float32)
    return d

def reference(tab_words, tab_scales, offs, pos1, pos2, pos3, w1, base, w2_words, w2_scales, gain, w3, hs):
    v = unpack_weight(tab_words, tab_scales, "e4m3")[:, unstriped(offs)]
    h = np.maximum(mxq(f64(w1), 0, "e4m3").T @ v, f64(base))
    z = h[:, unstriped(pos1)] + h[:, unstriped(pos2)]
    w2 = unpack_weight(w2_words, w2_scales, "e2m1")
    b = f64(gain)[:, None] * np.tanh(w2.T @ mxq(z, 0, "e4m3"))
    y = mxq(f64(w3), 0, "e4m3").T @ mxq(b, 0, "e4m3")
    diff = y[:, unstriped(pos3)] - f64(hs)[:, None] * h
    return np.sqrt(1.0 + np.square(diff))

@@ -1,0 +1,296 @@
+from contextlib import ExitStack
+
+import concourse.mybir as mybir
+
+K, T, S, BAYS, H = 1024, 2048, 1024, 512, 1024
+FLOPS = 2 * (K * H * S + H * H * BAYS + H * H * BAYS)
+
+F32 = mybir.dt.float32
+BF16 = mybir.dt.bfloat16
+I32 = mybir.dt.int32
+U32 = mybir.dt.uint32
+U16 = mybir.dt.uint16
+U8 = mybir.dt.uint8
+FP8X4 = mybir.dt.float8_e4m3fn_x4
+FP4X4 = mybir.dt.float4_e2m1fn_x4
+ALU = mybir.AluOpType
+ACT = mybir.ActivationFunctionType
+
+P = 128
+PACK = 4
+PASS = P * PACK
+PASSES = 2
+TILES = PASSES * PACK
+BANK = 512
+CHUNK = 128
+CHUNKS = BAYS // CHUNK
+PICK = 256
+PER_COL = 16
+
+
+def tile_list_hull_fouling_contrast_kernel(
+    tc, tab_words, tab_scales, offs, pos1, pos2, pos3, w1, base, w2_words, w2_scales, gain, w3, hs, out
+):
+    nc = tc.nc
+    with ExitStack() as ctx:
+        lists = ctx.enter_context(tc.tile_pool(name="lists", bufs=1))
+        keep = ctx.enter_context(tc.tile_pool(name="keep", bufs=1))
+        ring = ctx.enter_context(tc.tile_pool(name="ring", bufs=1))
+        psum = ctx.enter_context(tc.psum_pool(name="psum", bufs=4))
+
+        def rows_of(matrix, i):
+            b, t = divmod(i, PACK)
+            return matrix[b * PASS : (b + 1) * PASS, :].rearrange("(p t) n -> p t n", t=PACK)[:, t, :]
+
+        def load_list(src, name):
+            tile = lists.tile(list(src.shape), U16, name=name)
+            nc.sync.dma_start(tile[:], src)
+            return tile
+
+        def load_weight(w, a, b, name):
+            raw = ring.tile([P, PACK, PASS], F32, name=name, tag="wide", bufs=4)
+            nc.sync.dma_start(
+                raw[:], w[a * PASS : (a + 1) * PASS, b * PASS : (b + 1) * PASS].rearrange("(p j) c -> p j c", j=PACK)
+            )
+            return raw
+
+        def round_weight(copy, raw, name, tag="rounded", bufs=3):
+            rounded = ring.tile([P, PACK * PASS], BF16, name=name, tag=tag, bufs=bufs, align_bytes=64)
+            copy(
+                rounded[:].rearrange("p (t m j) -> p m j t", t=PACK, j=PACK),
+                raw[:].rearrange("p j (m t) -> p m j t", t=PACK),
+            )
+            return rounded
+
+        def quantize_weight(rounded, name, codes=None):
+            if codes is None:
+                codes = keep.tile([P, PASS], U32, name=name + "_codes", align_bytes=64)
+            scales = keep.tile([P, PASS], U8, name=name + "_scales", align_bytes=64)
+            nc.vector.quantize_mx(out=codes[:].bitcast(FP8X4), scales=scales[:], in_=rounded[:])
+            return codes, scales
+
+        tab_plane = keep.tile([P, T], U8, name="tab_plane", align_bytes=64)
+        w2_plane = keep.tile([P, PASSES, H], U8, name="w2_plane", align_bytes=64)
+        nc.vector.memset(tab_plane[:].bitcast(I32), 0)
+        nc.gpsimd.memset(w2_plane[:].bitcast(I32), 0)
+
+        offs_sb = load_list(offs, "offs_sb")
+        table = [keep.tile([P, T], I32, name="table%d" % a, align_bytes=64) for a in range(PASSES)]
+
+        def load_table(a):
+            nc.sync.dma_start(table[a][:], tab_words[a].rearrange("p n t -> p (n t)").bitcast(I32))
+
+        load_table(0)
+        for q in range(4):
+            nc.sync.dma_start(
+                tab_plane[32 * q : 32 * q + 4 * PASSES, :].bitcast(I32), tab_scales[:, 4 * q : 4 * q + 4, :].bitcast(I32)
+            )
+        w1_raw = {}
+        w1_raw[0, 0] = load_weight(w1, 0, 0, "w1_raw00")
+        load_table(1)
+        w1_raw[1, 0] = load_weight(w1, 1, 0, "w1_raw10")
+        floor = [keep.tile([P, S], F32, name="floor%d" % i) for i in range(TILES)]
+
+        def load_floor(i):
+            nc.sync.dma_start(floor[i][:], rows_of(base, i))
+
+        load_floor(0)
+        pos1_sb = load_list(pos1, "pos1_sb")
+        pos2_sb = load_list(pos2, "pos2_sb")
+        hs_sb = keep.tile([P, PASSES, PACK], F32, name="hs_sb")
+        nc.sync.dma_start(hs_sb[:], hs.rearrange("(b p t) -> p b t", b=PASSES, t=PACK))
+        for i in range(1, PACK):
+            load_floor(i)
+        for a in range(PASSES):
+            w1_raw[a, 1] = load_weight(w1, a, 1, "w1_raw%d1" % a)
+        w3_raw = {}
+        for a in range(PASSES):
+            w3_raw[a, 0] = load_weight(w3, a, 0, "w3_raw%d0" % a)
+        load_floor(PACK)
+        for q in range(4):
+            nc.sync.dma_start(
+                w2_plane[32 * q : 32 * q + 4, :, :].bitcast(I32),
+                w2_scales[:, 4 * q : 4 * q + 4, :].rearrange("a r c -> r a c").bitcast(I32),
+            )
+        w2_raw = keep.tile([P, PASSES, 2 * H], U8, name="w2_raw", align_bytes=64)
+        nc.sync.dma_start(w2_raw[:].bitcast(I32), w2_words.rearrange("a p c -> p a c").bitcast(I32))
+        gain_sb = keep.tile([P, PASSES, PACK], F32, name="gain_sb")
+        nc.sync.dma_start(gain_sb[:], gain.rearrange("(b p t) -> p b t", b=PASSES, t=PACK))
+        pos3_sb = load_list(pos3, "pos3_sb")
+        for a in range(PASSES):
+            w3_raw[a, 1] = load_weight(w3, a, 1, "w3_raw%d1" % a)
+        for i in range(PACK + 1, TILES):
+            load_floor(i)
+
+        picked = [keep.tile([P, S], U32, name="picked%d" % a, align_bytes=64) for a in range(PASSES)]
+        picked_plane = keep.tile([P, S], U8, name="picked_plane", align_bytes=64)
+        w1_mx = {}
+        nc.vector.tensor_copy(picked[0][:], table[0][:].bitcast(U32).indirect(offs_sb[:]))
+        nc.vector.tensor_copy(picked_plane[:], tab_plane[:].indirect(offs_sb[:]))
+        rounded = round_weight(nc.scalar.copy, w1_raw[0, 0], "w1_rounded00")
+        nc.vector.tensor_copy(picked[1][:], table[1][:].bitcast(U32).indirect(offs_sb[:]))
+        w1_mx[0, 0] = quantize_weight(rounded, "w1_00")
+        w1_mx[1, 0] = quantize_weight(round_weight(nc.vector.tensor_copy, w1_raw[1, 0], "w1_rounded10"), "w1_10")
+
+        h = [keep.tile([P, S], F32, name="h%d" % i) for i in range(TILES)]
+        z = [keep.tile([P, PACK, BAYS], F32, name="z%d" % b, align_bytes=64) for b in range(PASSES)]
+        z_codes = [keep.tile([P, BAYS], U32, name="z_codes%d" % b, align_bytes=64) for b in range(PASSES)]
+        z_scales = [keep.tile([P, BAYS], U8, name="z_scales%d" % b, align_bytes=64) for b in range(PASSES)]
+        first = {}
+
+        def features(i):
+            b, t = divmod(i, PACK)
+            for half in range(S // BANK):
+                cols = slice(half * BANK, (half + 1) * BANK)
+                acc = psum.tile([P, BANK], F32, name="acc_h", tag="acc")
+                for a in range(PASSES):
+                    codes, scales = w1_mx[a, b]
+                    nc.tensor.matmul_mx(
+                        out=acc[:],
+                        lhsT=codes[:, t * P : (t + 1) * P].bitcast(FP8X4),
+                        lhsT_scale=scales[:, t * P : (t + 1) * P],
+                        rhs=picked[a][:, cols].bitcast(FP8X4),
+                        rhs_scale=picked_plane[4 * a : P, cols],
+                        start=(a == 0),
+                        stop=(a == PASSES - 1),
+                    )
+                nc.vector.tensor_tensor(h[i][:, cols], acc[:], floor[i][:, cols], ALU.max)
+
+        def pick_first(i, lo, hi):
+            if i not in first:
+                first[i] = ring.tile([P, BAYS], F32, name="first", bufs=2, align_bytes=64)
+            nc.vector.tensor_copy(first[i][:, lo:hi], h[i][:].indirect(pos1_sb[:, lo // PER_COL : hi // PER_COL]))
+
+        def add_second(i, lo, hi):
+            b, t = divmod(i, PACK)
+            nc.vector.tensor_tensor(
+                z[b][:, t, lo:hi], h[i][:].indirect(pos2_sb[:, lo // PER_COL : hi // PER_COL]), first[i][:, lo:hi], ALU.add
+            )
+
+        def scale_features(i):
+            b, t = divmod(i, PACK)
+            nc.scalar.activation(floor[i][:], h[i][:], ACT.Copy, scale=hs_sb[:, b, t : t + 1])
+
+        def quantize_z(b, lo, hi):
+            woven = ring.tile([P, PACK * (hi - lo)], BF16, name="z_woven", tag="rounded", bufs=3, align_bytes=64)
+            nc.scalar.copy(
+                woven[:].rearrange("p (c i t) -> p c t i", i=4, t=PACK),
+                z[b][:, :, lo:hi].rearrange("p t (c i) -> p c t i", i=4),
+            )
+            nc.vector.quantize_mx(out=z_codes[b][:, lo:hi].bitcast(FP8X4), scales=z_scales[b][:, lo:hi], in_=woven[:])
+
+        last = TILES - 1
+        for i in range(TILES):
+            if i == 1:
+                for a in range(PASSES):
+                    w1_mx[a, 1] = quantize_weight(
+                        round_weight(nc.scalar.copy, w1_raw[a, 1], "w1_rounded%d1" % a), "w1_%d1" % a
+                    )
+            features(i)
+            if i > 0:
+                add_second(i - 1, 0, BAYS)
+            if i == PACK:
+                quantize_z(0, 0, BAYS)
+            if i < last:
+                pick_first(i, 0, BAYS)
+                scale_features(i)
+
+        w2_codes = keep.tile([P, PASSES * 2 * H], U8, name="w2_codes", align_bytes=64)
+        w2_dealt = keep.tile([P, PASSES * H], U8, name="w2_dealt", align_bytes=64)
+        nc.scalar.copy(
+            w2_codes[:].bitcast(U16).rearrange("p (g t q) -> p g t q", t=PACK, q=P),
+            w2_raw[:].rearrange("p a c -> p (a c)").bitcast(U16).rearrange("p (g q t) -> p g t q", t=PACK, q=P),
+        )
+        nc.gpsimd.tensor_copy(
+            w2_dealt[:].rearrange("p (g t q) -> p g t q", t=PACK, q=P),
+            w2_plane[:].rearrange("p a c -> p (a c)").rearrange("p (g q t) -> p g t q", t=PACK, q=P),
+        )
+
+        w3_mx = {}
+        w3_rounded = {}
+        for b in range(PASSES):
+            for a in range(PASSES):
+                w3_rounded[a, b] = round_weight(nc.scalar.copy, w3_raw[a, b], "w3_rounded%d%d" % (a, b), "w3_rounded", 4)
+
+        b_codes = [keep.tile([P, BAYS], U32, name="b_codes%d" % b, align_bytes=64) for b in range(PASSES)]
+        b_scales = [keep.tile([P, BAYS], U8, name="b_scales%d" % b, align_bytes=64) for b in range(PASSES)]
+        for c in range(CHUNKS):
+            pick_first(last, c * CHUNK, (c + 1) * CHUNK)
+        for c in range(CHUNKS):
+            add_second(last, c * CHUNK, (c + 1) * CHUNK)
+        for c in range(CHUNKS):
+            cols = slice(c * CHUNK, (c + 1) * CHUNK)
+            quantize_z(1, c * CHUNK, (c + 1) * CHUNK)
+            for b in range(PASSES):
+                acc = psum.tile([P, PACK, CHUNK], F32, name="acc_b")
+                for t in range(PACK):
+                    for a in range(PASSES):
+                        place = a * H + b * PASS + t * P
+                        nc.tensor.matmul_mx(
+                            out=acc[:, t, :],
+                            lhsT=w2_codes[:, 2 * place : 2 * (place + P)].bitcast(FP4X4),
+                            lhsT_scale=w2_dealt[:, place : place + P],
+                            rhs=z_codes[a][:, cols].bitcast(FP8X4),
+                            rhs_scale=z_scales[a][:, cols],
+                            start=(a == 0),
+                            stop=(a == PASSES - 1),
+                        )
+                bent = ring.tile([P, CHUNK, PACK], F32, name="bent", bufs=3)
+                nc.scalar.activation(bent[:], acc[:].rearrange("p t n -> p n t"), ACT.Tanh)
+                gained = ring.tile([P, CHUNK, PACK], BF16, name="gained", bufs=3, align_bytes=64)
+                nc.vector.tensor_tensor(
+                    gained[:], bent[:], gain_sb[:, b, :].unsqueeze(1).to_broadcast([P, CHUNK, PACK]), ALU.mult
+                )
+                nc.vector.quantize_mx(
+                    out=b_codes[b][:, cols].bitcast(FP8X4),
+                    scales=b_scales[b][:, cols],
+                    in_=gained[:].rearrange("p n t -> p (n t)"),
+                )
+        scale_features(last)
+        for a in range(PASSES):
+            codes = ring.tile([P, PASS], U32, name="w3_codes", tag="first", bufs=2, align_bytes=64)
+            w3_mx[a, 0] = quantize_weight(w3_rounded[a, 0], "w3_%d0" % a, codes)
+        late_codes = keep.tile([P, PASSES, PASS], U32, name="w3_late_codes", tag="z1", align_bytes=64)
+        for a in range(PASSES):
+            w3_mx[a, 1] = quantize_weight(w3_rounded[a, 1], "w3_%d1" % a, late_codes[:, a, :])
+
+        y = {}
+
+        def bays(i):
+            b, t = divmod(i, PACK)
+            acc = psum.tile([P, BAYS], F32, name="acc_y", tag="acc")
+            for a in range(PASSES):
+                codes, scales = w3_mx[a, b]
+                nc.tensor.matmul_mx(
+                    out=acc[:],
+                    lhsT=codes[:, t * P : (t + 1) * P].bitcast(FP8X4),
+                    lhsT_scale=scales[:, t * P : (t + 1) * P],
+                    rhs=b_codes[a][:].bitcast(FP8X4),
+                    rhs_scale=b_scales[a][:],
+                    start=(a == 0),
+                    stop=(a == PASSES - 1),
+                )
+            y[i] = ring.tile([P, BAYS], F32, name="y", bufs=4)
+            copy = nc.vector.tensor_copy if i % 2 == 0 else nc.scalar.copy
+            copy(y[i][:], acc[:])
+
+        def contrast(i, width):
+            diff = ring.tile([P, S], F32, name="diff", tag="wide", bufs=4)
+            for lo in range(0, S, PICK):
+                nc.vector.tensor_tensor(
+                    diff[:, lo : lo + PICK],
+                    y[i][:].indirect(pos3_sb[:, lo // PER_COL : (lo + PICK) // PER_COL]),
+                    floor[i][:, lo : lo + PICK],
+                    ALU.subtract,
+                )
+            for lo in range(0, S, width):
+                cols = slice(lo, lo + width)
+                nc.scalar.activation(diff[:, cols], diff[:, cols], ACT.Square)
+                nc.scalar.activation(floor[i][:, cols], diff[:, cols], ACT.Sqrt, bias=1.0)
+                nc.sync.dma_start(rows_of(out, i)[:, cols], floor[i][:, cols])
+
+        bays(0)
+        for i in range(TILES):
+            if i < last:
+                bays(i + 1)
+            contrast(i, S if i < last else PICK)

@@ -24,7 +24,7 @@ TILES = PASSES * PACK
 BANK = 512
 CHUNK = 128
 CHUNKS = BAYS // CHUNK
-PICK = 256
+PICKS = ((0, 352), (352, 704), (704, 1024))
 PER_COL = 16
 
 
@@ -54,20 +54,29 @@ def tile_list_hull_fouling_contrast_kernel(
             )
             return raw
 
-        def round_weight(copy, raw, name, tag="rounded", bufs=3):
-            rounded = ring.tile([P, PACK * PASS], BF16, name=name, tag=tag, bufs=bufs, align_bytes=64)
+        def round_weight(copy, raw, name, tag="rounded", bufs=3, lo=0, hi=PACK):
+            rounded = ring.tile([P, (hi - lo) * PASS], BF16, name=name, tag=tag, bufs=bufs, align_bytes=64)
             copy(
-                rounded[:].rearrange("p (t m j) -> p m j t", t=PACK, j=PACK),
-                raw[:].rearrange("p j (m t) -> p m j t", t=PACK),
+                rounded[:].rearrange("p (t m j) -> p m j t", m=P, j=PACK),
+                raw[:].rearrange("p j (m t) -> p m j t", t=PACK)[:, :, :, lo:hi],
             )
             return rounded
 
-        def quantize_weight(rounded, name, codes=None):
+        def weight_tiles(name, codes=None):
             if codes is None:
                 codes = keep.tile([P, PASS], U32, name=name + "_codes", align_bytes=64)
             scales = keep.tile([P, PASS], U8, name=name + "_scales", align_bytes=64)
-            nc.vector.quantize_mx(out=codes[:].bitcast(FP8X4), scales=scales[:], in_=rounded[:])
             return codes, scales
+
+        def quantize_into(tiles, rounded, lo=0, hi=PACK):
+            codes, scales = tiles
+            cols = slice(lo * P, hi * P)
+            nc.vector.quantize_mx(out=codes[:, cols].bitcast(FP8X4), scales=scales[:, cols], in_=rounded[:])
+
+        def quantize_weight(rounded, name, codes=None):
+            tiles = weight_tiles(name, codes)
+            quantize_into(tiles, rounded)
+            return tiles
 
         tab_plane = keep.tile([P, T], U8, name="tab_plane", align_bytes=64)
         w2_plane = keep.tile([P, PASSES, H], U8, name="w2_plane", align_bytes=64)
@@ -80,26 +89,32 @@ def tile_list_hull_fouling_contrast_kernel(
         def load_table(a):
             nc.sync.dma_start(table[a][:], tab_words[a].rearrange("p n t -> p (n t)").bitcast(I32))
 
-        load_table(0)
+        pos1_sb = load_list(pos1, "pos1_sb")
+        pos2_sb = load_list(pos2, "pos2_sb")
         for q in range(4):
             nc.sync.dma_start(
                 tab_plane[32 * q : 32 * q + 4 * PASSES, :].bitcast(I32), tab_scales[:, 4 * q : 4 * q + 4, :].bitcast(I32)
             )
+        for a in range(PASSES):
+            load_table(a)
+        for q in range(4):
+            nc.sync.dma_start(
+                w2_plane[32 * q : 32 * q + 4, :, :].bitcast(I32),
+                w2_scales[:, 4 * q : 4 * q + 4, :].rearrange("a r c -> r a c").bitcast(I32),
+            )
         w1_raw = {}
-        w1_raw[0, 0] = load_weight(w1, 0, 0, "w1_raw00")
-        load_table(1)
-        w1_raw[1, 0] = load_weight(w1, 1, 0, "w1_raw10")
+        for a in range(PASSES):
+            w1_raw[a, 0] = load_weight(w1, a, 0, "w1_raw%d0" % a)
         floor = [keep.tile([P, S], F32, name="floor%d" % i) for i in range(TILES)]
 
         def load_floor(i):
             nc.sync.dma_start(floor[i][:], rows_of(base, i))
 
         load_floor(0)
-        pos1_sb = load_list(pos1, "pos1_sb")
-        pos2_sb = load_list(pos2, "pos2_sb")
+        load_floor(1)
         hs_sb = keep.tile([P, PASSES, PACK], F32, name="hs_sb")
         nc.sync.dma_start(hs_sb[:], hs.rearrange("(b p t) -> p b t", b=PASSES, t=PACK))
-        for i in range(1, PACK):
+        for i in range(2, PACK):
             load_floor(i)
         for a in range(PASSES):
             w1_raw[a, 1] = load_weight(w1, a, 1, "w1_raw%d1" % a)
@@ -107,11 +122,6 @@ def tile_list_hull_fouling_contrast_kernel(
         for a in range(PASSES):
             w3_raw[a, 0] = load_weight(w3, a, 0, "w3_raw%d0" % a)
         load_floor(PACK)
-        for q in range(4):
-            nc.sync.dma_start(
-                w2_plane[32 * q : 32 * q + 4, :, :].bitcast(I32),
-                w2_scales[:, 4 * q : 4 * q + 4, :].rearrange("a r c -> r a c").bitcast(I32),
-            )
         w2_raw = keep.tile([P, PASSES, 2 * H], U8, name="w2_raw", align_bytes=64)
         nc.sync.dma_start(w2_raw[:].bitcast(I32), w2_words.rearrange("a p c -> p a c").bitcast(I32))
         gain_sb = keep.tile([P, PASSES, PACK], F32, name="gain_sb")
@@ -125,18 +135,30 @@ def tile_list_hull_fouling_contrast_kernel(
         picked = [keep.tile([P, S], U32, name="picked%d" % a, align_bytes=64) for a in range(PASSES)]
         picked_plane = keep.tile([P, S], U8, name="picked_plane", align_bytes=64)
         w1_mx = {}
-        nc.vector.tensor_copy(picked[0][:], table[0][:].bitcast(U32).indirect(offs_sb[:]))
         nc.vector.tensor_copy(picked_plane[:], tab_plane[:].indirect(offs_sb[:]))
-        rounded = round_weight(nc.scalar.copy, w1_raw[0, 0], "w1_rounded00")
-        nc.vector.tensor_copy(picked[1][:], table[1][:].bitcast(U32).indirect(offs_sb[:]))
-        w1_mx[0, 0] = quantize_weight(rounded, "w1_00")
-        w1_mx[1, 0] = quantize_weight(round_weight(nc.vector.tensor_copy, w1_raw[1, 0], "w1_rounded10"), "w1_10")
+        for a in range(PASSES):
+            nc.vector.tensor_copy(picked[a][:], table[a][:].bitcast(U32).indirect(offs_sb[:]))
+        for a in range(PASSES):
+            w1_mx[a, 0] = weight_tiles("w1_%d0" % a)
+        for lo in (0, 2):
+            for a in range(PASSES):
+                copy = nc.vector.tensor_copy if (a, lo) == (1, 0) else nc.scalar.copy
+                tag, bufs = ("head", 1) if lo == 0 else ("rounded", 3)
+                rounded = round_weight(copy, w1_raw[a, 0], "w1_rounded", tag, bufs, lo, lo + 2)
+                quantize_into(w1_mx[a, 0], rounded, lo, lo + 2)
+        w2_dealt = keep.tile([P, PASSES * H], U8, name="w2_dealt", align_bytes=64)
+        nc.vector.tensor_copy(
+            w2_dealt[:].rearrange("p (g t q) -> p g t q", t=PACK, q=P),
+            w2_plane[:].rearrange("p a c -> p (a c)").rearrange("p (g q t) -> p g t q", t=PACK, q=P),
+        )
 
         h = [keep.tile([P, S], F32, name="h%d" % i) for i in range(TILES)]
         z = [keep.tile([P, PACK, BAYS], F32, name="z%d" % b, align_bytes=64) for b in range(PASSES)]
         z_codes = [keep.tile([P, BAYS], U32, name="z_codes%d" % b, align_bytes=64) for b in range(PASSES)]
         z_scales = [keep.tile([P, BAYS], U8, name="z_scales%d" % b, align_bytes=64) for b in range(PASSES)]
         first = {}
+        minus_hs = keep.tile([P, PASSES, PACK], F32, name="minus_hs")
+        nc.scalar.activation(minus_hs[:], hs_sb[:], ACT.Copy, scale=-1.0)
 
         def features(i):
             b, t = divmod(i, PACK)
@@ -169,7 +191,7 @@ def tile_list_hull_fouling_contrast_kernel(
 
         def scale_features(i):
             b, t = divmod(i, PACK)
-            nc.scalar.activation(floor[i][:], h[i][:], ACT.Copy, scale=hs_sb[:, b, t : t + 1])
+            nc.scalar.activation(floor[i][:], h[i][:], ACT.Copy, scale=minus_hs[:, b, t : t + 1])
 
         def quantize_z(b, lo, hi):
             woven = ring.tile([P, PACK * (hi - lo)], BF16, name="z_woven", tag="rounded", bufs=3, align_bytes=64)
@@ -193,17 +215,12 @@ def tile_list_hull_fouling_contrast_kernel(
                 quantize_z(0, 0, BAYS)
             if i < last:
                 pick_first(i, 0, BAYS)
-                scale_features(i)
+            scale_features(i)
 
         w2_codes = keep.tile([P, PASSES * 2 * H], U8, name="w2_codes", align_bytes=64)
-        w2_dealt = keep.tile([P, PASSES * H], U8, name="w2_dealt", align_bytes=64)
         nc.scalar.copy(
             w2_codes[:].bitcast(U16).rearrange("p (g t q) -> p g t q", t=PACK, q=P),
             w2_raw[:].rearrange("p a c -> p (a c)").bitcast(U16).rearrange("p (g q t) -> p g t q", t=PACK, q=P),
-        )
-        nc.gpsimd.tensor_copy(
-            w2_dealt[:].rearrange("p (g t q) -> p g t q", t=PACK, q=P),
-            w2_plane[:].rearrange("p a c -> p (a c)").rearrange("p (g q t) -> p g t q", t=PACK, q=P),
         )
 
         w3_mx = {}
@@ -212,15 +229,16 @@ def tile_list_hull_fouling_contrast_kernel(
             for a in range(PASSES):
                 w3_rounded[a, b] = round_weight(nc.scalar.copy, w3_raw[a, b], "w3_rounded%d%d" % (a, b), "w3_rounded", 4)
 
-        b_codes = [keep.tile([P, BAYS], U32, name="b_codes%d" % b, align_bytes=64) for b in range(PASSES)]
-        b_scales = [keep.tile([P, BAYS], U8, name="b_scales%d" % b, align_bytes=64) for b in range(PASSES)]
-        for c in range(CHUNKS):
-            pick_first(last, c * CHUNK, (c + 1) * CHUNK)
+        b_codes = [keep.tile([P, PASSES * CHUNK], U32, name="b_codes%d" % c, align_bytes=64) for c in range(CHUNKS)]
+        b_scales = [keep.tile([P, PASSES * CHUNK], U8, name="b_scales%d" % c, align_bytes=64) for c in range(CHUNKS)]
+        for lo in range(0, BAYS, BAYS // 2):
+            pick_first(last, lo, lo + BAYS // 2)
         for c in range(CHUNKS):
             add_second(last, c * CHUNK, (c + 1) * CHUNK)
         for c in range(CHUNKS):
             cols = slice(c * CHUNK, (c + 1) * CHUNK)
             quantize_z(1, c * CHUNK, (c + 1) * CHUNK)
+            bent = ring.tile([P, PASSES, CHUNK, PACK], F32, name="bent", bufs=2)
             for b in range(PASSES):
                 acc = psum.tile([P, PACK, CHUNK], F32, name="acc_b")
                 for t in range(PACK):
@@ -235,18 +253,14 @@ def tile_list_hull_fouling_contrast_kernel(
                             start=(a == 0),
                             stop=(a == PASSES - 1),
                         )
-                bent = ring.tile([P, CHUNK, PACK], F32, name="bent", bufs=3)
-                nc.scalar.activation(bent[:], acc[:].rearrange("p t n -> p n t"), ACT.Tanh)
-                gained = ring.tile([P, CHUNK, PACK], BF16, name="gained", bufs=3, align_bytes=64)
-                nc.vector.tensor_tensor(
-                    gained[:], bent[:], gain_sb[:, b, :].unsqueeze(1).to_broadcast([P, CHUNK, PACK]), ALU.mult
-                )
-                nc.vector.quantize_mx(
-                    out=b_codes[b][:, cols].bitcast(FP8X4),
-                    scales=b_scales[b][:, cols],
-                    in_=gained[:].rearrange("p n t -> p (n t)"),
-                )
-        scale_features(last)
+                nc.scalar.activation(bent[:, b], acc[:].rearrange("p t n -> p n t"), ACT.Tanh)
+            gained = ring.tile([P, PASSES, CHUNK, PACK], BF16, name="gained", bufs=2, align_bytes=64)
+            nc.vector.tensor_tensor(
+                gained[:], bent[:], gain_sb[:].unsqueeze(2).to_broadcast([P, PASSES, CHUNK, PACK]), ALU.mult
+            )
+            nc.vector.quantize_mx(
+                out=b_codes[c][:].bitcast(FP8X4), scales=b_scales[c][:], in_=gained[:].rearrange("p b n t -> p (b n t)")
+            )
         for a in range(PASSES):
             codes = ring.tile([P, PASS], U32, name="w3_codes", tag="first", bufs=2, align_bytes=64)
             w3_mx[a, 0] = quantize_weight(w3_rounded[a, 0], "w3_%d0" % a, codes)
@@ -254,43 +268,42 @@ def tile_list_hull_fouling_contrast_kernel(
         for a in range(PASSES):
             w3_mx[a, 1] = quantize_weight(w3_rounded[a, 1], "w3_%d1" % a, late_codes[:, a, :])
 
-        y = {}
+        y = [keep.tile([P, BAYS], F32, name="y%d" % i) for i in range(TILES)]
 
-        def bays(i):
-            b, t = divmod(i, PACK)
-            acc = psum.tile([P, BAYS], F32, name="acc_y", tag="acc")
-            for a in range(PASSES):
-                codes, scales = w3_mx[a, b]
-                nc.tensor.matmul_mx(
-                    out=acc[:],
-                    lhsT=codes[:, t * P : (t + 1) * P].bitcast(FP8X4),
-                    lhsT_scale=scales[:, t * P : (t + 1) * P],
-                    rhs=b_codes[a][:].bitcast(FP8X4),
-                    rhs_scale=b_scales[a][:],
-                    start=(a == 0),
-                    stop=(a == PASSES - 1),
-                )
-            y[i] = ring.tile([P, BAYS], F32, name="y", bufs=4)
-            copy = nc.vector.tensor_copy if i % 2 == 0 else nc.scalar.copy
-            copy(y[i][:], acc[:])
+        def bays(pair, half):
+            acc = psum.tile([P, 2, BAYS // 2], F32, name="acc_y", tag="acc")
+            for side in range(2):
+                b, t = divmod(2 * pair + side, PACK)
+                for step in range(2):
+                    c = 2 * half + step
+                    for a in range(PASSES):
+                        codes, scales = w3_mx[a, b]
+                        nc.tensor.matmul_mx(
+                            out=acc[:, side, step * CHUNK : (step + 1) * CHUNK],
+                            lhsT=codes[:, t * P : (t + 1) * P].bitcast(FP8X4),
+                            lhsT_scale=scales[:, t * P : (t + 1) * P],
+                            rhs=b_codes[c][:, a * CHUNK : (a + 1) * CHUNK].bitcast(FP8X4),
+                            rhs_scale=b_scales[c][:, a * CHUNK : (a + 1) * CHUNK],
+                            start=(a == 0),
+                            stop=(a == PASSES - 1),
+                        )
+            for side in range(2):
+                nc.scalar.copy(y[2 * pair + side][:, half * (BAYS // 2) : (half + 1) * (BAYS // 2)], acc[:, side, :])
 
         def contrast(i, width):
             diff = ring.tile([P, S], F32, name="diff", tag="wide", bufs=4)
-            for lo in range(0, S, PICK):
+            for lo, hi in PICKS:
                 nc.vector.tensor_tensor(
-                    diff[:, lo : lo + PICK],
-                    y[i][:].indirect(pos3_sb[:, lo // PER_COL : (lo + PICK) // PER_COL]),
-                    floor[i][:, lo : lo + PICK],
-                    ALU.subtract,
+                    diff[:, lo:hi], y[i][:].indirect(pos3_sb[:, lo // PER_COL : hi // PER_COL]), floor[i][:, lo:hi], ALU.add
                 )
-            for lo in range(0, S, width):
-                cols = slice(lo, lo + width)
+            for lo, hi in width:
+                cols = slice(lo, hi)
                 nc.scalar.activation(diff[:, cols], diff[:, cols], ACT.Square)
                 nc.scalar.activation(floor[i][:, cols], diff[:, cols], ACT.Sqrt, bias=1.0)
                 nc.sync.dma_start(rows_of(out, i)[:, cols], floor[i][:, cols])
 
-        bays(0)
+        for half in range(2):
+            for pair in range(TILES // 2):
+                bays(pair, half)
         for i in range(TILES):
-            if i < last:
-                bays(i + 1)
-            contrast(i, S if i < last else PICK)
+            contrast(i, ((0, S),) if 0 < i < last - 1 else PICKS)

@@ -36,6 +36,7 @@ def tile_list_hull_fouling_contrast_kernel(
         lists = ctx.enter_context(tc.tile_pool(name="lists", bufs=1))
         keep = ctx.enter_context(tc.tile_pool(name="keep", bufs=1))
         ring = ctx.enter_context(tc.tile_pool(name="ring", bufs=1))
+        head = ctx.enter_context(tc.tile_pool(name="head", bufs=1))
         psum = ctx.enter_context(tc.psum_pool(name="psum", bufs=4))
 
         def rows_of(matrix, i):
@@ -54,12 +55,15 @@ def tile_list_hull_fouling_contrast_kernel(
             )
             return raw
 
-        def round_weight(copy, raw, name, tag="rounded", bufs=3, lo=0, hi=PACK):
-            rounded = ring.tile([P, (hi - lo) * PASS], BF16, name=name, tag=tag, bufs=bufs, align_bytes=64)
+        def round_into(copy, rounded, raw, lo=0, hi=PACK):
             copy(
                 rounded[:].rearrange("p (t m j) -> p m j t", m=P, j=PACK),
                 raw[:].rearrange("p j (m t) -> p m j t", t=PACK)[:, :, :, lo:hi],
             )
+
+        def round_weight(copy, raw, name, tag="rounded", bufs=3, lo=0, hi=PACK):
+            rounded = ring.tile([P, (hi - lo) * PASS], BF16, name=name, tag=tag, bufs=bufs, align_bytes=64)
+            round_into(copy, rounded, raw, lo, hi)
             return rounded
 
         def weight_tiles(name, codes=None):
@@ -79,7 +83,7 @@ def tile_list_hull_fouling_contrast_kernel(
             return tiles
 
         tab_plane = keep.tile([P, T], U8, name="tab_plane", align_bytes=64)
-        w2_plane = keep.tile([P, PASSES, H], U8, name="w2_plane", align_bytes=64)
+        w2_plane = head.tile([P, PASSES, H], U8, name="w2_plane", align_bytes=64, offset=0)
         nc.vector.memset(tab_plane[:].bitcast(I32), 0)
         nc.gpsimd.memset(w2_plane[:].bitcast(I32), 0)
 
@@ -140,17 +144,17 @@ def tile_list_hull_fouling_contrast_kernel(
             nc.vector.tensor_copy(picked[a][:], table[a][:].bitcast(U32).indirect(offs_sb[:]))
         for a in range(PASSES):
             w1_mx[a, 0] = weight_tiles("w1_%d0" % a)
-        for lo in (0, 2):
-            for a in range(PASSES):
-                copy = nc.vector.tensor_copy if (a, lo) == (1, 0) else nc.scalar.copy
-                tag, bufs = ("head", 1) if lo == 0 else ("rounded", 3)
-                rounded = round_weight(copy, w1_raw[a, 0], "w1_rounded", tag, bufs, lo, lo + 2)
-                quantize_into(w1_mx[a, 0], rounded, lo, lo + 2)
         w2_dealt = keep.tile([P, PASSES * H], U8, name="w2_dealt", align_bytes=64)
         nc.vector.tensor_copy(
             w2_dealt[:].rearrange("p (g t q) -> p g t q", t=PACK, q=P),
             w2_plane[:].rearrange("p a c -> p (a c)").rearrange("p (g q t) -> p g t q", t=PACK, q=P),
         )
+        for a, copy, offset in ((0, nc.scalar.copy, 2048), (1, nc.vector.tensor_copy, 1024)):
+            rounded = head.tile([P, 2 * PASS], BF16, name="w1_head%d" % a, align_bytes=64, offset=offset)
+            round_into(copy, rounded, w1_raw[a, 0], 0, 2)
+            quantize_into(w1_mx[a, 0], rounded, 0, 2)
+        for a in range(PASSES):
+            quantize_into(w1_mx[a, 0], round_weight(nc.scalar.copy, w1_raw[a, 0], "w1_rounded", lo=2, hi=PACK), 2, PACK)
 
         h = [keep.tile([P, S], F32, name="h%d" % i) for i in range(TILES)]
         z = [keep.tile([P, PACK, BAYS], F32, name="z%d" % b, align_bytes=64) for b in range(PASSES)]
@@ -241,8 +245,8 @@ def tile_list_hull_fouling_contrast_kernel(
             bent = ring.tile([P, PASSES, CHUNK, PACK], F32, name="bent", bufs=2)
             for b in range(PASSES):
                 acc = psum.tile([P, PACK, CHUNK], F32, name="acc_b")
-                for t in range(PACK):
-                    for a in range(PASSES):
+                for a in range(PASSES):
+                    for t in range(PACK):
                         place = a * H + b * PASS + t * P
                         nc.tensor.matmul_mx(
                             out=acc[:, t, :],
@@ -250,8 +254,8 @@ def tile_list_hull_fouling_contrast_kernel(
                             lhsT_scale=w2_dealt[:, place : place + P],
                             rhs=z_codes[a][:, cols].bitcast(FP8X4),
                             rhs_scale=z_scales[a][:, cols],
-                            start=(a == 0),
-                            stop=(a == PASSES - 1),
+                            start=(a == 0 and t == 0),
+                            stop=(a == PASSES - 1 and t == PACK - 1),
                         )
                 nc.scalar.activation(bent[:, b], acc[:].rearrange("p t n -> p n t"), ACT.Tanh)
             gained = ring.tile([P, PASSES, CHUNK, PACK], BF16, name="gained", bufs=2, align_bytes=64)
@@ -298,7 +302,10 @@ def tile_list_hull_fouling_contrast_kernel(
                 )
             for lo, hi in width:
                 cols = slice(lo, hi)
-                nc.scalar.activation(diff[:, cols], diff[:, cols], ACT.Square)
+                if i == last:
+                    nc.vector.tensor_tensor(diff[:, cols], diff[:, cols], diff[:, cols], ALU.mult)
+                else:
+                    nc.scalar.activation(diff[:, cols], diff[:, cols], ACT.Square)
                 nc.scalar.activation(floor[i][:, cols], diff[:, cols], ACT.Sqrt, bias=1.0)
                 nc.sync.dma_start(rows_of(out, i)[:, cols], floor[i][:, cols])
 

@@ -25,6 +25,7 @@ BANK = 512
 CHUNK = 128
 CHUNKS = BAYS // CHUNK
 PICKS = ((0, 352), (352, 704), (704, 1024))
+LAST_PICKS = ((0, 352), (352, 704), (704, 896), (896, 1024))
 PER_COL = 16
 
 
@@ -63,7 +64,8 @@ def tile_list_hull_fouling_contrast_kernel(
 
         def round_weight(copy, raw, name, tag="rounded", bufs=3, lo=0, hi=PACK):
             rounded = ring.tile([P, (hi - lo) * PASS], BF16, name=name, tag=tag, bufs=bufs, align_bytes=64)
-            round_into(copy, rounded, raw, lo, hi)
+            for at in range(lo, hi, 2):
+                round_into(copy, rounded[:, (at - lo) * PASS : (at - lo + 2) * PASS], raw, at, at + 2)
             return rounded
 
         def weight_tiles(name, codes=None):
@@ -169,7 +171,8 @@ def tile_list_hull_fouling_contrast_kernel(
             for half in range(S // BANK):
                 cols = slice(half * BANK, (half + 1) * BANK)
                 acc = psum.tile([P, BANK], F32, name="acc_h", tag="acc")
-                for a in range(PASSES):
+                order = (0, 1) if i == 0 else (1, 0)
+                for a in order:
                     codes, scales = w1_mx[a, b]
                     nc.tensor.matmul_mx(
                         out=acc[:],
@@ -177,8 +180,8 @@ def tile_list_hull_fouling_contrast_kernel(
                         lhsT_scale=scales[:, t * P : (t + 1) * P],
                         rhs=picked[a][:, cols].bitcast(FP8X4),
                         rhs_scale=picked_plane[4 * a : P, cols],
-                        start=(a == 0),
-                        stop=(a == PASSES - 1),
+                        start=(a == order[0]),
+                        stop=(a == order[-1]),
                     )
                 nc.vector.tensor_tensor(h[i][:, cols], acc[:], floor[i][:, cols], ALU.max)
 
@@ -259,12 +262,19 @@ def tile_list_hull_fouling_contrast_kernel(
                         )
                 nc.scalar.activation(bent[:, b], acc[:].rearrange("p t n -> p n t"), ACT.Tanh)
             gained = ring.tile([P, PASSES, CHUNK, PACK], BF16, name="gained", bufs=2, align_bytes=64)
-            nc.vector.tensor_tensor(
-                gained[:], bent[:], gain_sb[:].unsqueeze(2).to_broadcast([P, PASSES, CHUNK, PACK]), ALU.mult
-            )
-            nc.vector.quantize_mx(
-                out=b_codes[c][:].bitcast(FP8X4), scales=b_scales[c][:], in_=gained[:].rearrange("p b n t -> p (b n t)")
-            )
+            step = PASSES if c < CHUNKS - 1 else 1
+            for b in range(0, PASSES, step):
+                part = slice(b, b + step)
+                nc.vector.tensor_tensor(
+                    gained[:, part], bent[:, part], gain_sb[:, part].unsqueeze(2).to_broadcast([P, step, CHUNK, PACK]), ALU.mult
+                )
+            for b in range(0, PASSES, step):
+                words = slice(b * CHUNK, (b + step) * CHUNK)
+                nc.vector.quantize_mx(
+                    out=b_codes[c][:, words].bitcast(FP8X4),
+                    scales=b_scales[c][:, words],
+                    in_=gained[:, b : b + step].rearrange("p b n t -> p (b n t)"),
+                )
         for a in range(PASSES):
             codes = ring.tile([P, PASS], U32, name="w3_codes", tag="first", bufs=2, align_bytes=64)
             w3_mx[a, 0] = quantize_weight(w3_rounded[a, 0], "w3_%d0" % a, codes)
@@ -296,7 +306,7 @@ def tile_list_hull_fouling_contrast_kernel(
 
         def contrast(i, width):
             diff = ring.tile([P, S], F32, name="diff", tag="wide", bufs=4)
-            for lo, hi in PICKS:
+            for lo, hi in PICKS if i < last else LAST_PICKS:
                 nc.vector.tensor_tensor(
                     diff[:, lo:hi], y[i][:].indirect(pos3_sb[:, lo // PER_COL : hi // PER_COL]), floor[i][:, lo:hi], ALU.add
                 )
@@ -313,4 +323,4 @@ def tile_list_hull_fouling_contrast_kernel(
             for pair in range(TILES // 2):
                 bays(pair, half)
         for i in range(TILES):
-            contrast(i, ((0, S),) if 0 < i < last - 1 else PICKS)
+            contrast(i, ((0, S),) if 0 < i < last - 1 else PICKS if i < last else LAST_PICKS)

@@ -21,12 +21,15 @@ PACK = 4
 PASS = P * PACK
 PASSES = 2
 TILES = PASSES * PACK
+PAIR = 2
 BANK = 512
+QUADRANTS = 4
 CHUNK = 128
 CHUNKS = BAYS // CHUNK
-PICKS = ((0, 352), (352, 704), (704, 1024))
-LAST_PICKS = ((0, 352), (352, 704), (704, 896), (896, 1024))
+HALF = BAYS // 2
 PER_COL = 16
+PICKS = ((0, 352), (352, 704), (704, S))
+LAST_PICKS = ((0, 352), (352, 704), (704, 896), (896, S))
 
 
 def tile_list_hull_fouling_contrast_kernel(
@@ -37,7 +40,6 @@ def tile_list_hull_fouling_contrast_kernel(
         lists = ctx.enter_context(tc.tile_pool(name="lists", bufs=1))
         keep = ctx.enter_context(tc.tile_pool(name="keep", bufs=1))
         ring = ctx.enter_context(tc.tile_pool(name="ring", bufs=1))
-        head = ctx.enter_context(tc.tile_pool(name="head", bufs=1))
         psum = ctx.enter_context(tc.psum_pool(name="psum", bufs=4))
 
         def rows_of(matrix, i):
@@ -56,16 +58,16 @@ def tile_list_hull_fouling_contrast_kernel(
             )
             return raw
 
-        def round_into(copy, rounded, raw, lo=0, hi=PACK):
+        def round_into(copy, rounded, raw, lo, hi):
             copy(
-                rounded[:].rearrange("p (t m j) -> p m j t", m=P, j=PACK),
-                raw[:].rearrange("p j (m t) -> p m j t", t=PACK)[:, :, :, lo:hi],
+                rounded[:].rearrange("p (t q j) -> p q j t", q=P, j=PACK),
+                raw[:].rearrange("p j (q t) -> p q j t", t=PACK)[:, :, :, lo:hi],
             )
 
-        def round_weight(copy, raw, name, tag="rounded", bufs=3, lo=0, hi=PACK):
-            rounded = ring.tile([P, (hi - lo) * PASS], BF16, name=name, tag=tag, bufs=bufs, align_bytes=64)
-            for at in range(lo, hi, 2):
-                round_into(copy, rounded[:, (at - lo) * PASS : (at - lo + 2) * PASS], raw, at, at + 2)
+        def round_weight(raw, name, tag="rounded", bufs=3, lo=0):
+            rounded = ring.tile([P, (PACK - lo) * PASS], BF16, name=name, tag=tag, bufs=bufs, align_bytes=64)
+            for at in range(lo, PACK, PAIR):
+                round_into(nc.scalar.copy, rounded[:, (at - lo) * PASS : (at - lo + PAIR) * PASS], raw, at, at + PAIR)
             return rounded
 
         def weight_tiles(name, codes=None):
@@ -85,42 +87,36 @@ def tile_list_hull_fouling_contrast_kernel(
             return tiles
 
         tab_plane = keep.tile([P, T], U8, name="tab_plane", align_bytes=64)
-        w2_plane = head.tile([P, PASSES, H], U8, name="w2_plane", align_bytes=64, offset=0)
+        w2_plane = keep.tile([P, PASSES, H], U8, name="w2_plane", align_bytes=64)
         nc.vector.memset(tab_plane[:].bitcast(I32), 0)
         nc.gpsimd.memset(w2_plane[:].bitcast(I32), 0)
 
         offs_sb = load_list(offs, "offs_sb")
         table = [keep.tile([P, T], I32, name="table%d" % a, align_bytes=64) for a in range(PASSES)]
-
-        def load_table(a):
-            nc.sync.dma_start(table[a][:], tab_words[a].rearrange("p n t -> p (n t)").bitcast(I32))
-
         pos1_sb = load_list(pos1, "pos1_sb")
         pos2_sb = load_list(pos2, "pos2_sb")
-        for q in range(4):
+        for quad in range(QUADRANTS):
             nc.sync.dma_start(
-                tab_plane[32 * q : 32 * q + 4 * PASSES, :].bitcast(I32), tab_scales[:, 4 * q : 4 * q + 4, :].bitcast(I32)
+                tab_plane[32 * quad : 32 * quad + 4 * PASSES, :].bitcast(I32),
+                tab_scales[:, 4 * quad : 4 * quad + 4, :].bitcast(I32),
             )
         for a in range(PASSES):
-            load_table(a)
-        for q in range(4):
-            nc.sync.dma_start(
-                w2_plane[32 * q : 32 * q + 4, :, :].bitcast(I32),
-                w2_scales[:, 4 * q : 4 * q + 4, :].rearrange("a r c -> r a c").bitcast(I32),
-            )
+            nc.sync.dma_start(table[a][:], tab_words[a].rearrange("p n t -> p (n t)").bitcast(I32))
         w1_raw = {}
         for a in range(PASSES):
             w1_raw[a, 0] = load_weight(w1, a, 0, "w1_raw%d0" % a)
         floor = [keep.tile([P, S], F32, name="floor%d" % i) for i in range(TILES)]
+        minus_hs_h = floor
+        result = floor
 
         def load_floor(i):
             nc.sync.dma_start(floor[i][:], rows_of(base, i))
 
-        load_floor(0)
-        load_floor(1)
+        for i in range(PAIR):
+            load_floor(i)
         hs_sb = keep.tile([P, PASSES, PACK], F32, name="hs_sb")
         nc.sync.dma_start(hs_sb[:], hs.rearrange("(b p t) -> p b t", b=PASSES, t=PACK))
-        for i in range(2, PACK):
+        for i in range(PAIR, PACK):
             load_floor(i)
         for a in range(PASSES):
             w1_raw[a, 1] = load_weight(w1, a, 1, "w1_raw%d1" % a)
@@ -128,6 +124,11 @@ def tile_list_hull_fouling_contrast_kernel(
         for a in range(PASSES):
             w3_raw[a, 0] = load_weight(w3, a, 0, "w3_raw%d0" % a)
         load_floor(PACK)
+        for quad in range(QUADRANTS):
+            nc.sync.dma_start(
+                w2_plane[32 * quad : 32 * quad + 4, :, :].bitcast(I32),
+                w2_scales[:, 4 * quad : 4 * quad + 4, :].rearrange("a r c -> r a c").bitcast(I32),
+            )
         w2_raw = keep.tile([P, PASSES, 2 * H], U8, name="w2_raw", align_bytes=64)
         nc.sync.dma_start(w2_raw[:].bitcast(I32), w2_words.rearrange("a p c -> p a c").bitcast(I32))
         gain_sb = keep.tile([P, PASSES, PACK], F32, name="gain_sb")
@@ -146,17 +147,12 @@ def tile_list_hull_fouling_contrast_kernel(
             nc.vector.tensor_copy(picked[a][:], table[a][:].bitcast(U32).indirect(offs_sb[:]))
         for a in range(PASSES):
             w1_mx[a, 0] = weight_tiles("w1_%d0" % a)
-        w2_dealt = keep.tile([P, PASSES * H], U8, name="w2_dealt", align_bytes=64)
-        nc.vector.tensor_copy(
-            w2_dealt[:].rearrange("p (g t q) -> p g t q", t=PACK, q=P),
-            w2_plane[:].rearrange("p a c -> p (a c)").rearrange("p (g q t) -> p g t q", t=PACK, q=P),
-        )
-        for a, copy, offset in ((0, nc.scalar.copy, 2048), (1, nc.vector.tensor_copy, 1024)):
-            rounded = head.tile([P, 2 * PASS], BF16, name="w1_head%d" % a, align_bytes=64, offset=offset)
-            round_into(copy, rounded, w1_raw[a, 0], 0, 2)
-            quantize_into(w1_mx[a, 0], rounded, 0, 2)
+        for a, copy in enumerate((nc.scalar.copy, nc.vector.tensor_copy)):
+            rounded = ring.tile([P, PAIR * PASS], BF16, name="w1_head", align_bytes=64)
+            round_into(copy, rounded, w1_raw[a, 0], 0, PAIR)
+            quantize_into(w1_mx[a, 0], rounded, 0, PAIR)
         for a in range(PASSES):
-            quantize_into(w1_mx[a, 0], round_weight(nc.scalar.copy, w1_raw[a, 0], "w1_rounded", lo=2, hi=PACK), 2, PACK)
+            quantize_into(w1_mx[a, 0], round_weight(w1_raw[a, 0], "w1_rounded", lo=PAIR), PAIR, PACK)
 
         h = [keep.tile([P, S], F32, name="h%d" % i) for i in range(TILES)]
         z = [keep.tile([P, PACK, BAYS], F32, name="z%d" % b, align_bytes=64) for b in range(PASSES)]
@@ -198,7 +194,7 @@ def tile_list_hull_fouling_contrast_kernel(
 
         def scale_features(i):
             b, t = divmod(i, PACK)
-            nc.scalar.activation(floor[i][:], h[i][:], ACT.Copy, scale=minus_hs[:, b, t : t + 1])
+            nc.scalar.activation(minus_hs_h[i][:], h[i][:], ACT.Copy, scale=minus_hs[:, b, t : t + 1])
 
         def quantize_z(b, lo, hi):
             woven = ring.tile([P, PACK * (hi - lo)], BF16, name="z_woven", tag="rounded", bufs=3, align_bytes=64)
@@ -212,9 +208,7 @@ def tile_list_hull_fouling_contrast_kernel(
         for i in range(TILES):
             if i == 1:
                 for a in range(PASSES):
-                    w1_mx[a, 1] = quantize_weight(
-                        round_weight(nc.scalar.copy, w1_raw[a, 1], "w1_rounded%d1" % a), "w1_%d1" % a
-                    )
+                    w1_mx[a, 1] = quantize_weight(round_weight(w1_raw[a, 1], "w1_rounded%d1" % a), "w1_%d1" % a)
             features(i)
             if i > 0:
                 add_second(i - 1, 0, BAYS)
@@ -230,16 +224,21 @@ def tile_list_hull_fouling_contrast_kernel(
             w2_raw[:].rearrange("p a c -> p (a c)").bitcast(U16).rearrange("p (g q t) -> p g t q", t=PACK, q=P),
         )
 
+        w2_dealt = keep.tile([P, PASSES * H], U8, name="w2_dealt", align_bytes=64)
+        nc.gpsimd.tensor_copy(
+            w2_dealt[:].rearrange("p (g t q) -> p g t q", t=PACK, q=P),
+            w2_plane[:].rearrange("p a c -> p (a c)").rearrange("p (g q t) -> p g t q", t=PACK, q=P),
+        )
         w3_mx = {}
         w3_rounded = {}
         for b in range(PASSES):
             for a in range(PASSES):
-                w3_rounded[a, b] = round_weight(nc.scalar.copy, w3_raw[a, b], "w3_rounded%d%d" % (a, b), "w3_rounded", 4)
+                w3_rounded[a, b] = round_weight(w3_raw[a, b], "w3_rounded%d%d" % (a, b), "w3_rounded", PASSES * PASSES)
 
         b_codes = [keep.tile([P, PASSES * CHUNK], U32, name="b_codes%d" % c, align_bytes=64) for c in range(CHUNKS)]
         b_scales = [keep.tile([P, PASSES * CHUNK], U8, name="b_scales%d" % c, align_bytes=64) for c in range(CHUNKS)]
-        for lo in range(0, BAYS, BAYS // 2):
-            pick_first(last, lo, lo + BAYS // 2)
+        for lo in range(0, BAYS, HALF):
+            pick_first(last, lo, lo + HALF)
         for c in range(CHUNKS):
             add_second(last, c * CHUNK, (c + 1) * CHUNK)
         for c in range(CHUNKS):
@@ -262,18 +261,17 @@ def tile_list_hull_fouling_contrast_kernel(
                         )
                 nc.scalar.activation(bent[:, b], acc[:].rearrange("p t n -> p n t"), ACT.Tanh)
             gained = ring.tile([P, PASSES, CHUNK, PACK], BF16, name="gained", bufs=2, align_bytes=64)
-            step = PASSES if c < CHUNKS - 1 else 1
-            for b in range(0, PASSES, step):
-                part = slice(b, b + step)
-                nc.vector.tensor_tensor(
-                    gained[:, part], bent[:, part], gain_sb[:, part].unsqueeze(2).to_broadcast([P, step, CHUNK, PACK]), ALU.mult
-                )
-            for b in range(0, PASSES, step):
-                words = slice(b * CHUNK, (b + step) * CHUNK)
+            blocks = PASSES if c < CHUNKS - 1 else 1
+            for b in range(0, PASSES, blocks):
+                part = slice(b, b + blocks)
+                gains = gain_sb[:, part].unsqueeze(2).to_broadcast([P, blocks, CHUNK, PACK])
+                nc.vector.tensor_tensor(gained[:, part], bent[:, part], gains, ALU.mult)
+            for b in range(0, PASSES, blocks):
+                words = slice(b * CHUNK, (b + blocks) * CHUNK)
                 nc.vector.quantize_mx(
                     out=b_codes[c][:, words].bitcast(FP8X4),
                     scales=b_scales[c][:, words],
-                    in_=gained[:, b : b + step].rearrange("p b n t -> p (b n t)"),
+                    in_=gained[:, b : b + blocks].rearrange("p b n t -> p (b n t)"),
                 )
         for a in range(PASSES):
             codes = ring.tile([P, PASS], U32, name="w3_codes", tag="first", bufs=2, align_bytes=64)
@@ -285,15 +283,15 @@ def tile_list_hull_fouling_contrast_kernel(
         y = [keep.tile([P, BAYS], F32, name="y%d" % i) for i in range(TILES)]
 
         def bays(pair, half):
-            acc = psum.tile([P, 2, BAYS // 2], F32, name="acc_y", tag="acc")
-            for side in range(2):
-                b, t = divmod(2 * pair + side, PACK)
-                for step in range(2):
-                    c = 2 * half + step
+            acc = psum.tile([P, PAIR, HALF], F32, name="acc_y", tag="acc")
+            for side in range(PAIR):
+                b, t = divmod(PAIR * pair + side, PACK)
+                for lo in range(0, HALF, CHUNK):
+                    c = (half * HALF + lo) // CHUNK
                     for a in range(PASSES):
                         codes, scales = w3_mx[a, b]
                         nc.tensor.matmul_mx(
-                            out=acc[:, side, step * CHUNK : (step + 1) * CHUNK],
+                            out=acc[:, side, lo : lo + CHUNK],
                             lhsT=codes[:, t * P : (t + 1) * P].bitcast(FP8X4),
                             lhsT_scale=scales[:, t * P : (t + 1) * P],
                             rhs=b_codes[c][:, a * CHUNK : (a + 1) * CHUNK].bitcast(FP8X4),
@@ -301,26 +299,26 @@ def tile_list_hull_fouling_contrast_kernel(
                             start=(a == 0),
                             stop=(a == PASSES - 1),
                         )
-            for side in range(2):
-                nc.scalar.copy(y[2 * pair + side][:, half * (BAYS // 2) : (half + 1) * (BAYS // 2)], acc[:, side, :])
+            for side in range(PAIR):
+                nc.scalar.copy(y[PAIR * pair + side][:, half * HALF : (half + 1) * HALF], acc[:, side, :])
 
-        def contrast(i, width):
+        def contrast(i):
+            picks = PICKS if i < last else LAST_PICKS
             diff = ring.tile([P, S], F32, name="diff", tag="wide", bufs=4)
-            for lo, hi in PICKS if i < last else LAST_PICKS:
-                nc.vector.tensor_tensor(
-                    diff[:, lo:hi], y[i][:].indirect(pos3_sb[:, lo // PER_COL : hi // PER_COL]), floor[i][:, lo:hi], ALU.add
-                )
-            for lo, hi in width:
+            for lo, hi in picks:
+                offsets = pos3_sb[:, lo // PER_COL : hi // PER_COL]
+                nc.vector.tensor_tensor(diff[:, lo:hi], y[i][:].indirect(offsets), minus_hs_h[i][:, lo:hi], ALU.add)
+            for lo, hi in ((0, S),) if 0 < i < last - 1 else picks:
                 cols = slice(lo, hi)
                 if i == last:
                     nc.vector.tensor_tensor(diff[:, cols], diff[:, cols], diff[:, cols], ALU.mult)
                 else:
                     nc.scalar.activation(diff[:, cols], diff[:, cols], ACT.Square)
-                nc.scalar.activation(floor[i][:, cols], diff[:, cols], ACT.Sqrt, bias=1.0)
-                nc.sync.dma_start(rows_of(out, i)[:, cols], floor[i][:, cols])
+                nc.scalar.activation(result[i][:, cols], diff[:, cols], ACT.Sqrt, bias=1.0)
+                nc.sync.dma_start(rows_of(out, i)[:, cols], result[i][:, cols])
 
-        for half in range(2):
-            for pair in range(TILES // 2):
+        for half in range(BAYS // HALF):
+            for pair in range(TILES // PAIR):
                 bays(pair, half)
         for i in range(TILES):
-            contrast(i, ((0, S),) if 0 < i < last - 1 else PICKS if i < last else LAST_PICKS)
+            contrast(i)

from contextlib import ExitStack

import concourse.mybir as mybir

K, T, S, BAYS, H = 1024, 2048, 1024, 512, 1024
FLOPS = 2 * (K * H * S + H * H * BAYS + H * H * BAYS)

F32 = mybir.dt.float32
BF16 = mybir.dt.bfloat16
I32 = mybir.dt.int32
U32 = mybir.dt.uint32
U16 = mybir.dt.uint16
U8 = mybir.dt.uint8
FP8X4 = mybir.dt.float8_e4m3fn_x4
FP4X4 = mybir.dt.float4_e2m1fn_x4
ALU = mybir.AluOpType
ACT = mybir.ActivationFunctionType

P = 128
PACK = 4
PASS = P * PACK
PASSES = 2
TILES = PASSES * PACK
PAIR = 2
BANK = 512
QUADRANTS = 4
CHUNK = 128
CHUNKS = BAYS // CHUNK
HALF = BAYS // 2
PER_COL = 16
PICKS = ((0, 352), (352, 704), (704, S))
LAST_PICKS = ((0, 352), (352, 704), (704, 896), (896, S))


def tile_list_hull_fouling_contrast_kernel(
    tc, tab_words, tab_scales, offs, pos1, pos2, pos3, w1, base, w2_words, w2_scales, gain, w3, hs, out
):
    nc = tc.nc
    with ExitStack() as ctx:
        lists = ctx.enter_context(tc.tile_pool(name="lists", bufs=1))
        keep = ctx.enter_context(tc.tile_pool(name="keep", bufs=1))
        ring = ctx.enter_context(tc.tile_pool(name="ring", bufs=1))
        psum = ctx.enter_context(tc.psum_pool(name="psum", bufs=4))

        def rows_of(matrix, i):
            b, t = divmod(i, PACK)
            return matrix[b * PASS : (b + 1) * PASS, :].rearrange("(p t) n -> p t n", t=PACK)[:, t, :]

        def load_list(src, name):
            tile = lists.tile(list(src.shape), U16, name=name)
            nc.sync.dma_start(tile[:], src)
            return tile

        def load_weight(w, a, b, name):
            raw = ring.tile([P, PACK, PASS], F32, name=name, tag="wide", bufs=4)
            nc.sync.dma_start(
                raw[:], w[a * PASS : (a + 1) * PASS, b * PASS : (b + 1) * PASS].rearrange("(p j) c -> p j c", j=PACK)
            )
            return raw

        def round_into(copy, rounded, raw, lo, hi):
            copy(
                rounded[:].rearrange("p (t q j) -> p q j t", q=P, j=PACK),
                raw[:].rearrange("p j (q t) -> p q j t", t=PACK)[:, :, :, lo:hi],
            )

        def round_weight(raw, name, tag="rounded", bufs=3, lo=0):
            rounded = ring.tile([P, (PACK - lo) * PASS], BF16, name=name, tag=tag, bufs=bufs, align_bytes=64)
            for at in range(lo, PACK, PAIR):
                round_into(nc.scalar.copy, rounded[:, (at - lo) * PASS : (at - lo + PAIR) * PASS], raw, at, at + PAIR)
            return rounded

        def weight_tiles(name, codes=None):
            if codes is None:
                codes = keep.tile([P, PASS], U32, name=name + "_codes", align_bytes=64)
            scales = keep.tile([P, PASS], U8, name=name + "_scales", align_bytes=64)
            return codes, scales

        def quantize_into(tiles, rounded, lo=0, hi=PACK):
            codes, scales = tiles
            cols = slice(lo * P, hi * P)
            nc.vector.quantize_mx(out=codes[:, cols].bitcast(FP8X4), scales=scales[:, cols], in_=rounded[:])

        def quantize_weight(rounded, name, codes=None):
            tiles = weight_tiles(name, codes)
            quantize_into(tiles, rounded)
            return tiles

        tab_plane = keep.tile([P, T], U8, name="tab_plane", align_bytes=64)
        w2_plane = keep.tile([P, PASSES, H], U8, name="w2_plane", align_bytes=64)
        nc.vector.memset(tab_plane[:].bitcast(I32), 0)
        nc.gpsimd.memset(w2_plane[:].bitcast(I32), 0)

        offs_sb = load_list(offs, "offs_sb")
        table = [keep.tile([P, T], I32, name="table%d" % a, align_bytes=64) for a in range(PASSES)]
        pos1_sb = load_list(pos1, "pos1_sb")
        pos2_sb = load_list(pos2, "pos2_sb")
        for quad in range(QUADRANTS):
            nc.sync.dma_start(
                tab_plane[32 * quad : 32 * quad + 4 * PASSES, :].bitcast(I32),
                tab_scales[:, 4 * quad : 4 * quad + 4, :].bitcast(I32),
            )
        for a in range(PASSES):
            nc.sync.dma_start(table[a][:], tab_words[a].rearrange("p n t -> p (n t)").bitcast(I32))
        w1_raw = {}
        for a in range(PASSES):
            w1_raw[a, 0] = load_weight(w1, a, 0, "w1_raw%d0" % a)
        floor = [keep.tile([P, S], F32, name="floor%d" % i) for i in range(TILES)]
        minus_hs_h = floor
        result = floor

        def load_floor(i):
            nc.sync.dma_start(floor[i][:], rows_of(base, i))

        for i in range(PAIR):
            load_floor(i)
        hs_sb = keep.tile([P, PASSES, PACK], F32, name="hs_sb")
        nc.sync.dma_start(hs_sb[:], hs.rearrange("(b p t) -> p b t", b=PASSES, t=PACK))
        for i in range(PAIR, PACK):
            load_floor(i)
        for a in range(PASSES):
            w1_raw[a, 1] = load_weight(w1, a, 1, "w1_raw%d1" % a)
        w3_raw = {}
        for a in range(PASSES):
            w3_raw[a, 0] = load_weight(w3, a, 0, "w3_raw%d0" % a)
        load_floor(PACK)
        for quad in range(QUADRANTS):
            nc.sync.dma_start(
                w2_plane[32 * quad : 32 * quad + 4, :, :].bitcast(I32),
                w2_scales[:, 4 * quad : 4 * quad + 4, :].rearrange("a r c -> r a c").bitcast(I32),
            )
        w2_raw = keep.tile([P, PASSES, 2 * H], U8, name="w2_raw", align_bytes=64)
        nc.sync.dma_start(w2_raw[:].bitcast(I32), w2_words.rearrange("a p c -> p a c").bitcast(I32))
        gain_sb = keep.tile([P, PASSES, PACK], F32, name="gain_sb")
        nc.sync.dma_start(gain_sb[:], gain.rearrange("(b p t) -> p b t", b=PASSES, t=PACK))
        pos3_sb = load_list(pos3, "pos3_sb")
        for a in range(PASSES):
            w3_raw[a, 1] = load_weight(w3, a, 1, "w3_raw%d1" % a)
        for i in range(PACK + 1, TILES):
            load_floor(i)

        picked = [keep.tile([P, S], U32, name="picked%d" % a, align_bytes=64) for a in range(PASSES)]
        picked_plane = keep.tile([P, S], U8, name="picked_plane", align_bytes=64)
        w1_mx = {}
        nc.vector.tensor_copy(picked_plane[:], tab_plane[:].indirect(offs_sb[:]))
        for a in range(PASSES):
            nc.vector.tensor_copy(picked[a][:], table[a][:].bitcast(U32).indirect(offs_sb[:]))
        for a in range(PASSES):
            w1_mx[a, 0] = weight_tiles("w1_%d0" % a)
        for a, copy in enumerate((nc.scalar.copy, nc.vector.tensor_copy)):
            rounded = ring.tile([P, PAIR * PASS], BF16, name="w1_head", align_bytes=64)
            round_into(copy, rounded, w1_raw[a, 0], 0, PAIR)
            quantize_into(w1_mx[a, 0], rounded, 0, PAIR)
        for a in range(PASSES):
            quantize_into(w1_mx[a, 0], round_weight(w1_raw[a, 0], "w1_rounded", lo=PAIR), PAIR, PACK)

        h = [keep.tile([P, S], F32, name="h%d" % i) for i in range(TILES)]
        z = [keep.tile([P, PACK, BAYS], F32, name="z%d" % b, align_bytes=64) for b in range(PASSES)]
        z_codes = [keep.tile([P, BAYS], U32, name="z_codes%d" % b, align_bytes=64) for b in range(PASSES)]
        z_scales = [keep.tile([P, BAYS], U8, name="z_scales%d" % b, align_bytes=64) for b in range(PASSES)]
        first = {}
        minus_hs = keep.tile([P, PASSES, PACK], F32, name="minus_hs")
        nc.scalar.activation(minus_hs[:], hs_sb[:], ACT.Copy, scale=-1.0)

        def features(i):
            b, t = divmod(i, PACK)
            for half in range(S // BANK):
                cols = slice(half * BANK, (half + 1) * BANK)
                acc = psum.tile([P, BANK], F32, name="acc_h", tag="acc")
                order = (0, 1) if i == 0 else (1, 0)
                for a in order:
                    codes, scales = w1_mx[a, b]
                    nc.tensor.matmul_mx(
                        out=acc[:],
                        lhsT=codes[:, t * P : (t + 1) * P].bitcast(FP8X4),
                        lhsT_scale=scales[:, t * P : (t + 1) * P],
                        rhs=picked[a][:, cols].bitcast(FP8X4),
                        rhs_scale=picked_plane[4 * a : P, cols],
                        start=(a == order[0]),
                        stop=(a == order[-1]),
                    )
                nc.vector.tensor_tensor(h[i][:, cols], acc[:], floor[i][:, cols], ALU.max)

        def pick_first(i, lo, hi):
            if i not in first:
                first[i] = ring.tile([P, BAYS], F32, name="first", bufs=2, align_bytes=64)
            nc.vector.tensor_copy(first[i][:, lo:hi], h[i][:].indirect(pos1_sb[:, lo // PER_COL : hi // PER_COL]))

        def add_second(i, lo, hi):
            b, t = divmod(i, PACK)
            nc.vector.tensor_tensor(
                z[b][:, t, lo:hi], h[i][:].indirect(pos2_sb[:, lo // PER_COL : hi // PER_COL]), first[i][:, lo:hi], ALU.add
            )

        def scale_features(i):
            b, t = divmod(i, PACK)
            nc.scalar.activation(minus_hs_h[i][:], h[i][:], ACT.Copy, scale=minus_hs[:, b, t : t + 1])

        def quantize_z(b, lo, hi):
            woven = ring.tile([P, PACK * (hi - lo)], BF16, name="z_woven", tag="rounded", bufs=3, align_bytes=64)
            nc.scalar.copy(
                woven[:].rearrange("p (c i t) -> p c t i", i=4, t=PACK),
                z[b][:, :, lo:hi].rearrange("p t (c i) -> p c t i", i=4),
            )
            nc.vector.quantize_mx(out=z_codes[b][:, lo:hi].bitcast(FP8X4), scales=z_scales[b][:, lo:hi], in_=woven[:])

        last = TILES - 1
        for i in range(TILES):
            if i == 1:
                for a in range(PASSES):
                    w1_mx[a, 1] = quantize_weight(round_weight(w1_raw[a, 1], "w1_rounded%d1" % a), "w1_%d1" % a)
            features(i)
            if i > 0:
                add_second(i - 1, 0, BAYS)
            if i == PACK:
                quantize_z(0, 0, BAYS)
            if i < last:
                pick_first(i, 0, BAYS)
            scale_features(i)

        w2_codes = keep.tile([P, PASSES * 2 * H], U8, name="w2_codes", align_bytes=64)
        nc.scalar.copy(
            w2_codes[:].bitcast(U16).rearrange("p (g t q) -> p g t q", t=PACK, q=P),
            w2_raw[:].rearrange("p a c -> p (a c)").bitcast(U16).rearrange("p (g q t) -> p g t q", t=PACK, q=P),
        )

        w2_dealt = keep.tile([P, PASSES * H], U8, name="w2_dealt", align_bytes=64)
        nc.gpsimd.tensor_copy(
            w2_dealt[:].rearrange("p (g t q) -> p g t q", t=PACK, q=P),
            w2_plane[:].rearrange("p a c -> p (a c)").rearrange("p (g q t) -> p g t q", t=PACK, q=P),
        )
        w3_mx = {}
        w3_rounded = {}
        for b in range(PASSES):
            for a in range(PASSES):
                w3_rounded[a, b] = round_weight(w3_raw[a, b], "w3_rounded%d%d" % (a, b), "w3_rounded", PASSES * PASSES)

        b_codes = [keep.tile([P, PASSES * CHUNK], U32, name="b_codes%d" % c, align_bytes=64) for c in range(CHUNKS)]
        b_scales = [keep.tile([P, PASSES * CHUNK], U8, name="b_scales%d" % c, align_bytes=64) for c in range(CHUNKS)]
        for lo in range(0, BAYS, HALF):
            pick_first(last, lo, lo + HALF)
        for c in range(CHUNKS):
            add_second(last, c * CHUNK, (c + 1) * CHUNK)
        for c in range(CHUNKS):
            cols = slice(c * CHUNK, (c + 1) * CHUNK)
            quantize_z(1, c * CHUNK, (c + 1) * CHUNK)
            bent = ring.tile([P, PASSES, CHUNK, PACK], F32, name="bent", bufs=2)
            for b in range(PASSES):
                acc = psum.tile([P, PACK, CHUNK], F32, name="acc_b")
                for a in range(PASSES):
                    for t in range(PACK):
                        place = a * H + b * PASS + t * P
                        nc.tensor.matmul_mx(
                            out=acc[:, t, :],
                            lhsT=w2_codes[:, 2 * place : 2 * (place + P)].bitcast(FP4X4),
                            lhsT_scale=w2_dealt[:, place : place + P],
                            rhs=z_codes[a][:, cols].bitcast(FP8X4),
                            rhs_scale=z_scales[a][:, cols],
                            start=(a == 0 and t == 0),
                            stop=(a == PASSES - 1 and t == PACK - 1),
                        )
                nc.scalar.activation(bent[:, b], acc[:].rearrange("p t n -> p n t"), ACT.Tanh)
            gained = ring.tile([P, PASSES, CHUNK, PACK], BF16, name="gained", bufs=2, align_bytes=64)
            blocks = PASSES if c < CHUNKS - 1 else 1
            for b in range(0, PASSES, blocks):
                part = slice(b, b + blocks)
                gains = gain_sb[:, part].unsqueeze(2).to_broadcast([P, blocks, CHUNK, PACK])
                nc.vector.tensor_tensor(gained[:, part], bent[:, part], gains, ALU.mult)
            for b in range(0, PASSES, blocks):
                words = slice(b * CHUNK, (b + blocks) * CHUNK)
                nc.vector.quantize_mx(
                    out=b_codes[c][:, words].bitcast(FP8X4),
                    scales=b_scales[c][:, words],
                    in_=gained[:, b : b + blocks].rearrange("p b n t -> p (b n t)"),
                )
        for a in range(PASSES):
            codes = ring.tile([P, PASS], U32, name="w3_codes", tag="first", bufs=2, align_bytes=64)
            w3_mx[a, 0] = quantize_weight(w3_rounded[a, 0], "w3_%d0" % a, codes)
        late_codes = keep.tile([P, PASSES, PASS], U32, name="w3_late_codes", tag="z1", align_bytes=64)
        for a in range(PASSES):
            w3_mx[a, 1] = quantize_weight(w3_rounded[a, 1], "w3_%d1" % a, late_codes[:, a, :])

        y = [keep.tile([P, BAYS], F32, name="y%d" % i) for i in range(TILES)]

        def bays(pair, half):
            acc = psum.tile([P, PAIR, HALF], F32, name="acc_y", tag="acc")
            for side in range(PAIR):
                b, t = divmod(PAIR * pair + side, PACK)
                for lo in range(0, HALF, CHUNK):
                    c = (half * HALF + lo) // CHUNK
                    for a in range(PASSES):
                        codes, scales = w3_mx[a, b]
                        nc.tensor.matmul_mx(
                            out=acc[:, side, lo : lo + CHUNK],
                            lhsT=codes[:, t * P : (t + 1) * P].bitcast(FP8X4),
                            lhsT_scale=scales[:, t * P : (t + 1) * P],
                            rhs=b_codes[c][:, a * CHUNK : (a + 1) * CHUNK].bitcast(FP8X4),
                            rhs_scale=b_scales[c][:, a * CHUNK : (a + 1) * CHUNK],
                            start=(a == 0),
                            stop=(a == PASSES - 1),
                        )
            for side in range(PAIR):
                nc.scalar.copy(y[PAIR * pair + side][:, half * HALF : (half + 1) * HALF], acc[:, side, :])

        def contrast(i):
            picks = PICKS if i < last else LAST_PICKS
            diff = ring.tile([P, S], F32, name="diff", tag="wide", bufs=4)
            for lo, hi in picks:
                offsets = pos3_sb[:, lo // PER_COL : hi // PER_COL]
                nc.vector.tensor_tensor(diff[:, lo:hi], y[i][:].indirect(offsets), minus_hs_h[i][:, lo:hi], ALU.add)
            for lo, hi in ((0, S),) if 0 < i < last - 1 else picks:
                cols = slice(lo, hi)
                if i == last:
                    nc.vector.tensor_tensor(diff[:, cols], diff[:, cols], diff[:, cols], ALU.mult)
                else:
                    nc.scalar.activation(diff[:, cols], diff[:, cols], ACT.Square)
                nc.scalar.activation(result[i][:, cols], diff[:, cols], ACT.Sqrt, bias=1.0)
                nc.sync.dma_start(rows_of(out, i)[:, cols], result[i][:, cols])

        for half in range(BAYS // HALF):
            for pair in range(TILES // PAIR):
                bays(pair, half)
        for i in range(TILES):
            contrast(i)
